import numpy as np
import ml_dtypes


def mxq(x, axis, fmt="e4m3"):
    dtype, down = {"e4m3": (ml_dtypes.float8_e4m3fn, 7), "e5m2": (ml_dtypes.float8_e5m2, 14)}[fmt]
    v = np.moveaxis(np.asarray(x, np.float32).astype(ml_dtypes.bfloat16).astype(np.float64), axis, -1)
    blocks = v.reshape(v.shape[:-1] + (-1, 32))
    amax = np.abs(blocks).max(-1, keepdims=True)
    byte = np.maximum(np.where(amax > 0, np.frexp(amax)[1] - 1 + 127, 0) - down, 1)
    scale = np.exp2(byte - 127.0)
    codes = (blocks / scale).astype(np.float32).astype(dtype).astype(np.float64)
    return np.moveaxis((codes * scale).reshape(v.shape), -1, axis)


WIDE = False


def mx_kscale(k):
    if not WIDE:
        return np.ones(k)
    levels = np.array([10, -10, 5, -5, 0])
    if k % 512:
        return np.exp2(np.random.permutation(np.resize(levels, k // 32))).repeat(32)
    a = np.empty((k // 512, 16))
    for p in range(k // 512):
        a[p, :8] = np.random.permutation(np.resize(levels, 8))
        for g in range(8):
            far = levels[np.abs(levels - a[p, g]) >= 10]
            a[p, g + 8] = far[np.random.randint(len(far))]
    return np.exp2(a.ravel()).repeat(32)


def f64(x):
    return np.asarray(x).astype(np.float64)


def striped(idx):
    return np.tile(np.asarray(idx).reshape(-1, 16).T, (8, 1)).astype(np.uint16)


def unstriped(offs):
    return offs[:16].T.reshape(-1).astype(np.int64)


B, N, C, D, NQ = 1, 512, 2048, 1024, 128
SEG = 16


def eight(codes):
    return np.concatenate([codes[h].reshape(-1, 16).T for h in range(8)]).astype(np.uint16)


def uneight(offs):
    return np.stack([offs[16 * h:16 * h + 16].T.reshape(-1) for h in range(8)]).astype(np.int64)


def setup_inputs():
    n = np.random.standard_normal
    s = mx_kscale(D)[:, None]
    grid = lambda x: np.round(x * 32) / 32
    return {
        "qT": (n((B, D, NQ)) * s / np.sqrt(D)).astype(np.float32),
        "cb": (grid(n((D, C))) / s).astype(np.float32),
        "norm": np.tile(np.random.randint(32, 129, N) / 64.0, (128, 1)).astype(np.float32),
        "offs": eight(np.random.randint(0, C, (8, N))),
        "offs2": eight(np.random.randint(0, C, (8, N))),
    }


def reference(qT, cb, norm, offs, offs2):
    k = []
    for part, offs_ in enumerate((offs, offs2,)):
        codes = uneight(offs_)
        k += [f64(cb)[512 * part + 64 * h:512 * part + 64 * h + 64][:, codes[h]] for h in range(8)]
    k = np.concatenate(k) * f64(norm)[:1]
    a = mxq(f64(qT), 1, "e4m3").transpose(0, 2, 1) @ mxq(k, 0, "e4m3")
    return a.reshape(B, NQ, N // SEG, SEG).max(-1)

@@ -1,0 +1,128 @@
+from contextlib import ExitStack
+
+import concourse.mybir as mybir
+from concourse.masks import make_identity
+
+F32 = mybir.dt.float32
+BF16 = mybir.dt.bfloat16
+U32 = mybir.dt.uint32
+U16 = mybir.dt.uint16
+U8 = mybir.dt.uint8
+FP8X4 = mybir.dt.float8_e4m3fn_x4
+MULT = mybir.AluOpType.mult
+
+P = 128
+PACK = 4
+K_PASS = P * PACK
+D, NQ, N, C = 1024, 128, 512, 2048
+SEG = 16
+PASSES = D // K_PASS
+CHUNK = 256
+CHUNKS = N // CHUNK
+
+FLOPS = 2 * NQ * N * D
+
+
+def tile_attend_pq_max16_kernel(tc, qT, cb, norm, offs, offs2, out):
+    nc = tc.nc
+    with ExitStack() as ctx:
+        keep = ctx.enter_context(tc.tile_pool(name="keep", bufs=1))
+        psum = ctx.enter_context(tc.psum_pool(name="psum", bufs=1))
+
+        lists = [keep.tile([P, N // 16], U16, name=f"list{g}") for g in range(PASSES)]
+        planes = [[keep.tile([P, C], F32, name=f"plane{g}_{t}") for t in range(PACK)] for g in range(PASSES)]
+        q_raw = [keep.tile([P, PACK, NQ], F32, name=f"q_raw{g}") for g in range(PASSES)]
+        norm_col = keep.tile([P, PACK], F32, name="norm_col")
+
+        def load_plane(g, t):
+            rows = cb[g * K_PASS:(g + 1) * K_PASS, :].rearrange("(p t) c -> p t c", t=PACK)
+            nc.sync.dma_start(out=planes[g][t][:], in_=rows[:, t, :])
+
+        def load_q(g):
+            nc.sync.dma_start(out=q_raw[g][:], in_=qT[0, g * K_PASS:(g + 1) * K_PASS, :].rearrange("(p t) q -> p t q", t=PACK))
+
+        nc.scalar.dma_start(out=norm_col[:], in_=norm[0:1, :].rearrange("a (p x) -> (a p) x", x=PACK))
+        load_plane(0, 0)
+        nc.sync.dma_start(lists[0][:], offs)
+        load_plane(0, 1)
+        nc.sync.dma_start(lists[1][:], offs2)
+        load_plane(0, 2)
+        load_plane(0, 3)
+        load_q(0)
+        for t in range(PACK):
+            load_plane(1, t)
+        load_q(1)
+
+        ident = keep.tile([P, P], F32, name="ident")
+        make_identity(nc, ident[:])
+        norm_ps = psum.tile([P, PACK, P], F32, name="norm_ps")
+        for j in range(PACK):
+            nc.tensor.transpose(norm_ps[:, j, :], norm_col[:, j:j + 1].to_broadcast([P, P]), ident[:])
+        norm_all = keep.tile([P, N], F32, name="norm_all")
+        nc.vector.tensor_copy(out=norm_all[:].rearrange("p (m j) -> p m j", j=PACK), in_=norm_ps[:].rearrange("p j m -> p m j"))
+
+        q_codes = [keep.tile([P, NQ], U32, align_bytes=64, name=f"q_codes{g}") for g in range(PASSES)]
+        q_scales = [keep.tile([P, NQ], U8, align_bytes=64, name=f"q_scales{g}") for g in range(PASSES)]
+        q_bf = [keep.tile([P, NQ, PACK], BF16, align_bytes=64, name=f"q_bf{g}") for g in range(PASSES)]
+        k_f32 = [[keep.tile([P, PACK, CHUNK], F32, name=f"k_f32_{g}_{c}") for c in range(CHUNKS)] for g in range(PASSES)]
+        k_bf = [[keep.tile([P, CHUNK, PACK], BF16, align_bytes=64, name=f"k_bf{g}_{c}") for c in range(CHUNKS)] for g in range(PASSES)]
+        k_codes = [[keep.tile([P, CHUNK], U32, align_bytes=64, name=f"k_codes{g}_{c}") for c in range(CHUNKS)] for g in range(PASSES)]
+        k_scales = [[keep.tile([P, CHUNK], U8, align_bytes=64, name=f"k_scales{g}_{c}") for c in range(CHUNKS)] for g in range(PASSES)]
+        acc = [psum.tile([P, CHUNK], F32, name=f"acc{c}") for c in range(CHUNKS)]
+        best = keep.tile([P, N // SEG], F32, name="best")
+
+        def gather(g, t, c):
+            cols = slice(c * CHUNK // 16, (c + 1) * CHUNK // 16)
+            nc.vector.tensor_tensor(
+                k_f32[g][c][:, t, :], planes[g][t][:].indirect(lists[g][:, cols]),
+                norm_all[:, c * CHUNK:(c + 1) * CHUNK], MULT)
+
+        def round_pair(copy, g, c, t0):
+            copy(out=k_bf[g][c][:, :, t0:t0 + 2], in_=k_f32[g][c][:, t0:t0 + 2, :].rearrange("p t n -> p n t"))
+
+        def quantise_k(g, c):
+            nc.vector.quantize_mx(out=k_codes[g][c][:].bitcast(FP8X4), scales=k_scales[g][c][:],
+                                  in_=k_bf[g][c][:].rearrange("p n t -> p (n t)"))
+
+        def quantise_q(g):
+            nc.vector.quantize_mx(out=q_codes[g][:].bitcast(FP8X4), scales=q_scales[g][:],
+                                  in_=q_bf[g][:].rearrange("p n t -> p (n t)"))
+
+        def multiply(g, c):
+            nc.tensor.matmul_mx(out=acc[c][:], lhsT=q_codes[g][:].bitcast(FP8X4), lhsT_scale=q_scales[g][:],
+                                rhs=k_codes[g][c][:].bitcast(FP8X4), rhs_scale=k_scales[g][c][:],
+                                start=(g == 0), stop=(g == PASSES - 1))
+
+        for t in range(PACK):
+            for c in range(CHUNKS):
+                gather(0, t, c)
+        for c in range(CHUNKS):
+            nc.scalar.copy(out=k_bf[0][c][:], in_=k_f32[0][c][:].rearrange("p t n -> p n t"))
+        nc.scalar.copy(out=q_bf[0][:], in_=q_raw[0][:].rearrange("p t q -> p q t"))
+        for c in range(CHUNKS):
+            gather(1, 0, c)
+        for c in range(CHUNKS):
+            quantise_k(0, c)
+        quantise_q(0)
+        for c in range(CHUNKS):
+            multiply(0, c)
+        for c in range(CHUNKS):
+            gather(1, 1, c)
+        for c in range(CHUNKS):
+            round_pair(nc.scalar.copy, 1, c, 0)
+        for t in (2, 3):
+            for c in range(CHUNKS):
+                gather(1, t, c)
+        round_pair(nc.scalar.copy, 1, 0, 2)
+        round_pair(nc.vector.tensor_copy, 1, 1, 2)
+        nc.scalar.copy(out=q_bf[1][:], in_=q_raw[1][:].rearrange("p t q -> p q t"))
+        quantise_k(1, 0)
+        quantise_q(1)
+        quantise_k(1, 1)
+        for c in range(CHUNKS):
+            multiply(1, c)
+        for c in range(CHUNKS):
+            s = CHUNK // SEG
+            nc.vector.tensor_reduce(out=best[:, c * s:(c + 1) * s], in_=acc[c][:].rearrange("p (j s) -> p j s", s=SEG),
+                                    axis=mybir.AxisListType.X, op=mybir.AluOpType.max)
+        nc.sync.dma_start(out=out.rearrange("b q j -> (b q) j"), in_=best[:])

@@ -17,8 +17,9 @@ K_PASS = P * PACK
 D, NQ, N, C = 1024, 128, 512, 2048
 SEG = 16
 PASSES = D // K_PASS
-CHUNK = 256
-CHUNKS = N // CHUNK
+PIECE = 256
+TAIL = 128
+TAILS = N // TAIL
 
 FLOPS = 2 * NQ * N * D
 
@@ -42,8 +43,8 @@ def tile_attend_pq_max16_kernel(tc, qT, cb, norm, offs, offs2, out):
             nc.sync.dma_start(out=q_raw[g][:], in_=qT[0, g * K_PASS:(g + 1) * K_PASS, :].rearrange("(p t) q -> p t q", t=PACK))
 
         nc.scalar.dma_start(out=norm_col[:], in_=norm[0:1, :].rearrange("a (p x) -> (a p) x", x=PACK))
-        load_plane(0, 0)
         nc.sync.dma_start(lists[0][:], offs)
+        load_plane(0, 0)
         load_plane(0, 1)
         nc.sync.dma_start(lists[1][:], offs2)
         load_plane(0, 2)
@@ -64,65 +65,71 @@ def tile_attend_pq_max16_kernel(tc, qT, cb, norm, offs, offs2, out):
         q_codes = [keep.tile([P, NQ], U32, align_bytes=64, name=f"q_codes{g}") for g in range(PASSES)]
         q_scales = [keep.tile([P, NQ], U8, align_bytes=64, name=f"q_scales{g}") for g in range(PASSES)]
         q_bf = [keep.tile([P, NQ, PACK], BF16, align_bytes=64, name=f"q_bf{g}") for g in range(PASSES)]
-        k_f32 = [[keep.tile([P, PACK, CHUNK], F32, name=f"k_f32_{g}_{c}") for c in range(CHUNKS)] for g in range(PASSES)]
-        k_bf = [[keep.tile([P, CHUNK, PACK], BF16, align_bytes=64, name=f"k_bf{g}_{c}") for c in range(CHUNKS)] for g in range(PASSES)]
-        k_codes = [[keep.tile([P, CHUNK], U32, align_bytes=64, name=f"k_codes{g}_{c}") for c in range(CHUNKS)] for g in range(PASSES)]
-        k_scales = [[keep.tile([P, CHUNK], U8, align_bytes=64, name=f"k_scales{g}_{c}") for c in range(CHUNKS)] for g in range(PASSES)]
-        acc = [psum.tile([P, CHUNK], F32, name=f"acc{c}") for c in range(CHUNKS)]
+        k_f32 = [keep.tile([P, PACK, N], F32, name=f"k_f32_{g}") for g in range(PASSES)]
+        k_bf = [keep.tile([P, N, PACK], BF16, align_bytes=64, name=f"k_bf{g}") for g in range(PASSES)]
+        k_codes = [keep.tile([P, N], U32, align_bytes=64, name=f"k_codes{g}") for g in range(PASSES)]
+        k_scales = [keep.tile([P, N], U8, align_bytes=64, name=f"k_scales{g}") for g in range(PASSES)]
+        acc = [psum.tile([P, TAIL], F32, name=f"acc{c}") for c in range(TAILS)]
         best = keep.tile([P, N // SEG], F32, name="best")
 
-        def gather(g, t, c):
-            cols = slice(c * CHUNK // 16, (c + 1) * CHUNK // 16)
+        def gather(g, t, n0, width):
             nc.vector.tensor_tensor(
-                k_f32[g][c][:, t, :], planes[g][t][:].indirect(lists[g][:, cols]),
-                norm_all[:, c * CHUNK:(c + 1) * CHUNK], MULT)
+                k_f32[g][:, t, n0:n0 + width], planes[g][t][:].indirect(lists[g][:, n0 // 16:(n0 + width) // 16]),
+                norm_all[:, n0:n0 + width], MULT)
 
-        def round_pair(copy, g, c, t0):
-            copy(out=k_bf[g][c][:, :, t0:t0 + 2], in_=k_f32[g][c][:, t0:t0 + 2, :].rearrange("p t n -> p n t"))
+        def round_planes(copy, g, t0, t1, n0, width):
+            copy(out=k_bf[g][:, n0:n0 + width, t0:t1], in_=k_f32[g][:, t0:t1, n0:n0 + width].rearrange("p t n -> p n t"))
 
-        def quantise_k(g, c):
-            nc.vector.quantize_mx(out=k_codes[g][c][:].bitcast(FP8X4), scales=k_scales[g][c][:],
-                                  in_=k_bf[g][c][:].rearrange("p n t -> p (n t)"))
-
-        def quantise_q(g):
-            nc.vector.quantize_mx(out=q_codes[g][:].bitcast(FP8X4), scales=q_scales[g][:],
-                                  in_=q_bf[g][:].rearrange("p n t -> p (n t)"))
+        def quantise_k(g, n0, width):
+            nc.vector.quantize_mx(out=k_codes[g][:, n0:n0 + width].bitcast(FP8X4), scales=k_scales[g][:, n0:n0 + width],
+                                  in_=k_bf[g][:, n0:n0 + width, :].rearrange("p n t -> p (n t)"))
 
         def multiply(g, c):
+            k_cols = slice(c * TAIL, (c + 1) * TAIL)
             nc.tensor.matmul_mx(out=acc[c][:], lhsT=q_codes[g][:].bitcast(FP8X4), lhsT_scale=q_scales[g][:],
-                                rhs=k_codes[g][c][:].bitcast(FP8X4), rhs_scale=k_scales[g][c][:],
+                                rhs=k_codes[g][:, k_cols].bitcast(FP8X4), rhs_scale=k_scales[g][:, k_cols],
                                 start=(g == 0), stop=(g == PASSES - 1))
 
-        for t in range(PACK):
-            for c in range(CHUNKS):
-                gather(0, t, c)
-        for c in range(CHUNKS):
-            nc.scalar.copy(out=k_bf[0][c][:], in_=k_f32[0][c][:].rearrange("p t n -> p n t"))
-        nc.scalar.copy(out=q_bf[0][:], in_=q_raw[0][:].rearrange("p t q -> p q t"))
-        for c in range(CHUNKS):
-            gather(1, 0, c)
-        for c in range(CHUNKS):
-            quantise_k(0, c)
-        quantise_q(0)
-        for c in range(CHUNKS):
-            multiply(0, c)
-        for c in range(CHUNKS):
-            gather(1, 1, c)
-        for c in range(CHUNKS):
-            round_pair(nc.scalar.copy, 1, c, 0)
-        for t in (2, 3):
-            for c in range(CHUNKS):
-                gather(1, t, c)
-        round_pair(nc.scalar.copy, 1, 0, 2)
-        round_pair(nc.vector.tensor_copy, 1, 1, 2)
-        nc.scalar.copy(out=q_bf[1][:], in_=q_raw[1][:].rearrange("p t q -> p q t"))
-        quantise_k(1, 0)
-        quantise_q(1)
-        quantise_k(1, 1)
-        for c in range(CHUNKS):
-            multiply(1, c)
-        for c in range(CHUNKS):
-            s = CHUNK // SEG
+        def round_q(copy, g):
+            copy(out=q_bf[g][:], in_=q_raw[g][:].rearrange("p t q -> p q t"))
+
+        def quantise_q(g):
+            nc.vector.quantize_mx(out=q_codes[g][:].bitcast(FP8X4), scales=q_scales[g][:], in_=q_bf[g][:].rearrange("p q t -> p (q t)"))
+
+        def maxima(c):
+            s = TAIL // SEG
             nc.vector.tensor_reduce(out=best[:, c * s:(c + 1) * s], in_=acc[c][:].rearrange("p (j s) -> p j s", s=SEG),
                                     axis=mybir.AxisListType.X, op=mybir.AluOpType.max)
+
+        for t in range(PACK):
+            for n0 in range(0, N, PIECE):
+                gather(0, t, n0, PIECE)
+        for n0 in range(0, N, PIECE):
+            round_planes(nc.scalar.copy, 0, 0, PACK, n0, PIECE)
+        round_q(nc.scalar.copy, 0)
+        for n0 in range(0, N, PIECE):
+            gather(1, 0, n0, PIECE)
+        quantise_k(0, 0, N)
+        quantise_q(0)
+        for c in range(TAILS):
+            multiply(0, c)
+        for t in (1, 2):
+            for n0 in range(0, N, PIECE):
+                gather(1, t, n0, PIECE)
+            if t == 1:
+                for n0 in range(0, N, PIECE):
+                    round_planes(nc.scalar.copy, 1, 0, 2, n0, PIECE)
+        for c in range(TAILS):
+            gather(1, 3, c * TAIL, TAIL)
+            round_planes(nc.scalar.copy, 1, 2, 4, c * TAIL, TAIL)
+        quantise_k(1, 0, TAIL)
+        round_q(nc.vector.tensor_copy, 1)
+        quantise_k(1, TAIL, TAIL)
+        quantise_q(1)
+        quantise_k(1, 2 * TAIL, TAIL)
+        quantise_k(1, 3 * TAIL, TAIL)
+        for c in range(TAILS):
+            multiply(1, c)
+        for c in range(TAILS):
+            maxima(c)
         nc.sync.dma_start(out=out.rearrange("b q j -> (b q) j"), in_=best[:])

@@ -18,8 +18,7 @@ D, NQ, N, C = 1024, 128, 512, 2048
 SEG = 16
 PASSES = D // K_PASS
 PIECE = 256
-TAIL = 128
-TAILS = N // TAIL
+CHUNKS = ((0, 256), (256, 128), (384, 128))
 
 FLOPS = 2 * NQ * N * D
 
@@ -43,8 +42,8 @@ def tile_attend_pq_max16_kernel(tc, qT, cb, norm, offs, offs2, out):
             nc.sync.dma_start(out=q_raw[g][:], in_=qT[0, g * K_PASS:(g + 1) * K_PASS, :].rearrange("(p t) q -> p t q", t=PACK))
 
         nc.scalar.dma_start(out=norm_col[:], in_=norm[0:1, :].rearrange("a (p x) -> (a p) x", x=PACK))
-        nc.sync.dma_start(lists[0][:], offs)
         load_plane(0, 0)
+        nc.sync.dma_start(lists[0][:], offs)
         load_plane(0, 1)
         nc.sync.dma_start(lists[1][:], offs2)
         load_plane(0, 2)
@@ -69,7 +68,7 @@ def tile_attend_pq_max16_kernel(tc, qT, cb, norm, offs, offs2, out):
         k_bf = [keep.tile([P, N, PACK], BF16, align_bytes=64, name=f"k_bf{g}") for g in range(PASSES)]
         k_codes = [keep.tile([P, N], U32, align_bytes=64, name=f"k_codes{g}") for g in range(PASSES)]
         k_scales = [keep.tile([P, N], U8, align_bytes=64, name=f"k_scales{g}") for g in range(PASSES)]
-        acc = [psum.tile([P, TAIL], F32, name=f"acc{c}") for c in range(TAILS)]
+        acc = [psum.tile([P, width], F32, name=f"acc{n0}") for n0, width in CHUNKS]
         best = keep.tile([P, N // SEG], F32, name="best")
 
         def gather(g, t, n0, width):
@@ -85,7 +84,8 @@ def tile_attend_pq_max16_kernel(tc, qT, cb, norm, offs, offs2, out):
                                   in_=k_bf[g][:, n0:n0 + width, :].rearrange("p n t -> p (n t)"))
 
         def multiply(g, c):
-            k_cols = slice(c * TAIL, (c + 1) * TAIL)
+            n0, width = CHUNKS[c]
+            k_cols = slice(n0, n0 + width)
             nc.tensor.matmul_mx(out=acc[c][:], lhsT=q_codes[g][:].bitcast(FP8X4), lhsT_scale=q_scales[g][:],
                                 rhs=k_codes[g][:, k_cols].bitcast(FP8X4), rhs_scale=k_scales[g][:, k_cols],
                                 start=(g == 0), stop=(g == PASSES - 1))
@@ -97,8 +97,8 @@ def tile_attend_pq_max16_kernel(tc, qT, cb, norm, offs, offs2, out):
             nc.vector.quantize_mx(out=q_codes[g][:].bitcast(FP8X4), scales=q_scales[g][:], in_=q_bf[g][:].rearrange("p q t -> p (q t)"))
 
         def maxima(c):
-            s = TAIL // SEG
-            nc.vector.tensor_reduce(out=best[:, c * s:(c + 1) * s], in_=acc[c][:].rearrange("p (j s) -> p j s", s=SEG),
+            n0, width = CHUNKS[c]
+            nc.vector.tensor_reduce(out=best[:, n0 // SEG:(n0 + width) // SEG], in_=acc[c][:].rearrange("p (j s) -> p j s", s=SEG),
                                     axis=mybir.AxisListType.X, op=mybir.AluOpType.max)
 
         for t in range(PACK):
@@ -111,7 +111,7 @@ def tile_attend_pq_max16_kernel(tc, qT, cb, norm, offs, offs2, out):
             gather(1, 0, n0, PIECE)
         quantise_k(0, 0, N)
         quantise_q(0)
-        for c in range(TAILS):
+        for c in range(len(CHUNKS)):
             multiply(0, c)
         for t in (1, 2):
             for n0 in range(0, N, PIECE):
@@ -119,17 +119,17 @@ def tile_attend_pq_max16_kernel(tc, qT, cb, norm, offs, offs2, out):
             if t == 1:
                 for n0 in range(0, N, PIECE):
                     round_planes(nc.scalar.copy, 1, 0, 2, n0, PIECE)
-        for c in range(TAILS):
-            gather(1, 3, c * TAIL, TAIL)
-            round_planes(nc.scalar.copy, 1, 2, 4, c * TAIL, TAIL)
-        quantise_k(1, 0, TAIL)
-        round_q(nc.vector.tensor_copy, 1)
-        quantise_k(1, TAIL, TAIL)
+        for n0, width in CHUNKS:
+            gather(1, 3, n0, width)
+        round_q(nc.scalar.copy, 1)
+        round_planes(nc.scalar.copy, 1, 2, 4, 0, 256)
+        round_planes(nc.vector.tensor_copy, 1, 2, 4, 256, 128)
+        round_planes(nc.scalar.copy, 1, 2, 4, 384, 128)
         quantise_q(1)
-        quantise_k(1, 2 * TAIL, TAIL)
-        quantise_k(1, 3 * TAIL, TAIL)
-        for c in range(TAILS):
+        for n0, width in CHUNKS:
+            quantise_k(1, n0, width)
+        for c in range(len(CHUNKS)):
             multiply(1, c)
-        for c in range(TAILS):
+        for c in range(len(CHUNKS)):
             maxima(c)
         nc.sync.dma_start(out=out.rearrange("b q j -> (b q) j"), in_=best[:])

from contextlib import ExitStack

import concourse.mybir as mybir
from concourse.masks import make_identity

F32 = mybir.dt.float32
BF16 = mybir.dt.bfloat16
U32 = mybir.dt.uint32
U16 = mybir.dt.uint16
U8 = mybir.dt.uint8
FP8X4 = mybir.dt.float8_e4m3fn_x4
MULT = mybir.AluOpType.mult

P = 128
PACK = 4
K_PASS = P * PACK
D, NQ, N, C = 1024, 128, 512, 2048
SEG = 16
PASSES = D // K_PASS
PIECE = 256
CHUNKS = ((0, 256), (256, 128), (384, 128))

FLOPS = 2 * NQ * N * D


def tile_attend_pq_max16_kernel(tc, qT, cb, norm, offs, offs2, out):
    nc = tc.nc
    with ExitStack() as ctx:
        keep = ctx.enter_context(tc.tile_pool(name="keep", bufs=1))
        psum = ctx.enter_context(tc.psum_pool(name="psum", bufs=1))

        lists = [keep.tile([P, N // 16], U16, name=f"list{g}") for g in range(PASSES)]
        planes = [[keep.tile([P, C], F32, name=f"plane{g}_{t}") for t in range(PACK)] for g in range(PASSES)]
        q_raw = [keep.tile([P, PACK, NQ], F32, name=f"q_raw{g}") for g in range(PASSES)]
        norm_col = keep.tile([P, PACK], F32, name="norm_col")

        def load_plane(g, t):
            rows = cb[g * K_PASS:(g + 1) * K_PASS, :].rearrange("(p t) c -> p t c", t=PACK)
            nc.sync.dma_start(out=planes[g][t][:], in_=rows[:, t, :])

        def load_q(g):
            nc.sync.dma_start(out=q_raw[g][:], in_=qT[0, g * K_PASS:(g + 1) * K_PASS, :].rearrange("(p t) q -> p t q", t=PACK))

        nc.scalar.dma_start(out=norm_col[:], in_=norm[0:1, :].rearrange("a (p x) -> (a p) x", x=PACK))
        load_plane(0, 0)
        nc.sync.dma_start(lists[0][:], offs)
        load_plane(0, 1)
        nc.sync.dma_start(lists[1][:], offs2)
        load_plane(0, 2)
        load_plane(0, 3)
        load_q(0)
        for t in range(PACK):
            load_plane(1, t)
        load_q(1)

        ident = keep.tile([P, P], F32, name="ident")
        make_identity(nc, ident[:])
        norm_ps = psum.tile([P, PACK, P], F32, name="norm_ps")
        for j in range(PACK):
            nc.tensor.transpose(norm_ps[:, j, :], norm_col[:, j:j + 1].to_broadcast([P, P]), ident[:])
        norm_all = keep.tile([P, N], F32, name="norm_all")
        nc.vector.tensor_copy(out=norm_all[:].rearrange("p (m j) -> p m j", j=PACK), in_=norm_ps[:].rearrange("p j m -> p m j"))

        q_codes = [keep.tile([P, NQ], U32, align_bytes=64, name=f"q_codes{g}") for g in range(PASSES)]
        q_scales = [keep.tile([P, NQ], U8, align_bytes=64, name=f"q_scales{g}") for g in range(PASSES)]
        q_bf = [keep.tile([P, NQ, PACK], BF16, align_bytes=64, name=f"q_bf{g}") for g in range(PASSES)]
        k_f32 = [keep.tile([P, PACK, N], F32, name=f"k_f32_{g}") for g in range(PASSES)]
        k_bf = [keep.tile([P, N, PACK], BF16, align_bytes=64, name=f"k_bf{g}") for g in range(PASSES)]
        k_codes = [keep.tile([P, N], U32, align_bytes=64, name=f"k_codes{g}") for g in range(PASSES)]
        k_scales = [keep.tile([P, N], U8, align_bytes=64, name=f"k_scales{g}") for g in range(PASSES)]
        acc = [psum.tile([P, width], F32, name=f"acc{n0}") for n0, width in CHUNKS]
        best = keep.tile([P, N // SEG], F32, name="best")

        def gather(g, t, n0, width):
            nc.vector.tensor_tensor(
                k_f32[g][:, t, n0:n0 + width], planes[g][t][:].indirect(lists[g][:, n0 // 16:(n0 + width) // 16]),
                norm_all[:, n0:n0 + width], MULT)

        def round_planes(copy, g, t0, t1, n0, width):
            copy(out=k_bf[g][:, n0:n0 + width, t0:t1], in_=k_f32[g][:, t0:t1, n0:n0 + width].rearrange("p t n -> p n t"))

        def quantise_k(g, n0, width):
            nc.vector.quantize_mx(out=k_codes[g][:, n0:n0 + width].bitcast(FP8X4), scales=k_scales[g][:, n0:n0 + width],
                                  in_=k_bf[g][:, n0:n0 + width, :].rearrange("p n t -> p (n t)"))

        def multiply(g, c):
            n0, width = CHUNKS[c]
            k_cols = slice(n0, n0 + width)
            nc.tensor.matmul_mx(out=acc[c][:], lhsT=q_codes[g][:].bitcast(FP8X4), lhsT_scale=q_scales[g][:],
                                rhs=k_codes[g][:, k_cols].bitcast(FP8X4), rhs_scale=k_scales[g][:, k_cols],
                                start=(g == 0), stop=(g == PASSES - 1))

        def round_q(copy, g):
            copy(out=q_bf[g][:], in_=q_raw[g][:].rearrange("p t q -> p q t"))

        def quantise_q(g):
            nc.vector.quantize_mx(out=q_codes[g][:].bitcast(FP8X4), scales=q_scales[g][:], in_=q_bf[g][:].rearrange("p q t -> p (q t)"))

        def maxima(c):
            n0, width = CHUNKS[c]
            nc.vector.tensor_reduce(out=best[:, n0 // SEG:(n0 + width) // SEG], in_=acc[c][:].rearrange("p (j s) -> p j s", s=SEG),
                                    axis=mybir.AxisListType.X, op=mybir.AluOpType.max)

        for t in range(PACK):
            for n0 in range(0, N, PIECE):
                gather(0, t, n0, PIECE)
        for n0 in range(0, N, PIECE):
            round_planes(nc.scalar.copy, 0, 0, PACK, n0, PIECE)
        round_q(nc.scalar.copy, 0)
        for n0 in range(0, N, PIECE):
            gather(1, 0, n0, PIECE)
        quantise_k(0, 0, N)
        quantise_q(0)
        for c in range(len(CHUNKS)):
            multiply(0, c)
        for t in (1, 2):
            for n0 in range(0, N, PIECE):
                gather(1, t, n0, PIECE)
            if t == 1:
                for n0 in range(0, N, PIECE):
                    round_planes(nc.scalar.copy, 1, 0, 2, n0, PIECE)
        for n0, width in CHUNKS:
            gather(1, 3, n0, width)
        round_q(nc.scalar.copy, 1)
        round_planes(nc.scalar.copy, 1, 2, 4, 0, 256)
        round_planes(nc.vector.tensor_copy, 1, 2, 4, 256, 128)
        round_planes(nc.scalar.copy, 1, 2, 4, 384, 128)
        quantise_q(1)
        for n0, width in CHUNKS:
            quantise_k(1, n0, width)
        for c in range(len(CHUNKS)):
            multiply(1, c)
        for c in range(len(CHUNKS)):
            maxima(c)
        nc.sync.dma_start(out=out.rearrange("b q j -> (b q) j"), in_=best[:])
